import numpy as np
import ml_dtypes


def mxq(x, axis, fmt="e4m3"):
    dtype, down = {"e4m3": (ml_dtypes.float8_e4m3fn, 7), "e5m2": (ml_dtypes.float8_e5m2, 14)}[fmt]
    v = np.moveaxis(np.asarray(x, np.float32).astype(ml_dtypes.bfloat16).astype(np.float64), axis, -1)
    blocks = v.reshape(v.shape[:-1] + (-1, 32))
    amax = np.abs(blocks).max(-1, keepdims=True)
    byte = np.maximum(np.where(amax > 0, np.frexp(amax)[1] - 1 + 127, 0) - down, 1)
    scale = np.exp2(byte - 127.0)
    codes = (blocks / scale).astype(np.float32).astype(dtype).astype(np.float64)
    return np.moveaxis((codes * scale).reshape(v.shape), -1, axis)


WIDE = False


def mx_kscale(k):
    if not WIDE:
        return np.ones(k)
    levels = np.array([10, -10, 5, -5, 0])
    if k % 512:
        return np.exp2(np.random.permutation(np.resize(levels, k // 32))).repeat(32)
    a = np.empty((k // 512, 16))
    for p in range(k // 512):
        a[p, :8] = np.random.permutation(np.resize(levels, 8))
        for g in range(8):
            far = levels[np.abs(levels - a[p, g]) >= 10]
            a[p, g + 8] = far[np.random.randint(len(far))]
    return np.exp2(a.ravel()).repeat(32)


def f64(x):
    return np.asarray(x).astype(np.float64)


def striped(idx):
    return np.tile(idx.reshape(-1, 16).T, (8, 1)).astype(np.uint16)


def unstriped(offs):
    return offs[:16].T.reshape(-1).astype(np.int64)


E2M1 = np.array([0.0, 0.5, 1.0, 1.5, 2.0, 3.0, 4.0, 6.0, -0.0, -0.5, -1.0, -1.5, -2.0, -3.0, -4.0, -6.0])


def pack_weight(w, fmt):
    k, n = w.shape
    w = f64(np.asarray(w, np.float32).astype(ml_dtypes.bfloat16)).reshape(k // 32, 32, n)
    amax = np.abs(w).max(1)
    if fmt == "e4m3":
        byte = np.frexp(amax)[1] - 1 + 127 - 7
    else:
        mant, ex = np.frexp(amax / 6.0)
        byte = np.where(mant > 0.5, ex, ex - 1) + 127
    byte = np.clip(np.where(amax > 0, byte, 1), 1, 254)
    scaled = (w * np.exp2(127.0 - byte)[:, None, :]).reshape(k, n).astype(np.float32)
    by_word = np.ascontiguousarray(scaled.reshape(k // 512, 128, 4, n).transpose(0, 1, 3, 2))
    if fmt == "e4m3":
        words = by_word.astype(ml_dtypes.float8_e4m3fn).view(np.uint8)
    else:
        c = by_word.astype(ml_dtypes.float4_e2m1fn).view(np.uint8) & 0xF
        words = (c[..., 0::2] | (c[..., 1::2] << 4)).reshape(k // 512, 128, 2 * n)
    return np.ascontiguousarray(words), np.ascontiguousarray(byte.astype(np.uint8).reshape(k // 512, 16, n))


def unpack_weight(words, scales, fmt):
    g, _, n = scales.shape
    words = np.ascontiguousarray(words).reshape(g, 128, n, -1)
    if fmt == "e4m3":
        vals = words.view(ml_dtypes.float8_e4m3fn).astype(np.float64)
    else:
        nib = np.empty((g, 128, n, 4), np.uint8)
        nib[..., 0::2] = words & 0xF
        nib[..., 1::2] = words >> 4
        vals = E2M1[nib]
    vals = vals * np.repeat(np.exp2(scales.astype(np.float64) - 127.0), 8, axis=1)[..., None]
    return vals.transpose(0, 1, 3, 2).reshape(g * 512, n)


def gelu(v):
    return 0.5 * v * (1.0 + np.tanh(np.sqrt(2.0 / np.pi) * (v + 0.044715 * v**3)))


def bf(x):
    return np.asarray(x, np.float32).astype(ml_dtypes.bfloat16)


def planes(Y):
    n, m = Y.shape
    b = f64(bf(Y)).reshape(n // 32, 32, m)
    amax = np.abs(b).max(1)
    byte = np.clip(np.where(amax > 0, np.frexp(amax)[1] - 1 + 127 - 7, 1), 1, 254)
    codes = (b * np.exp2(127.0 - byte)[:, None, :]).reshape(n, m).astype(np.float32).astype(ml_dtypes.float8_e4m3fn).view(np.uint8)
    words = codes.reshape(n // 512, 128, 4, m).transpose(0, 1, 3, 2)
    return np.ascontiguousarray(words), np.ascontiguousarray(byte.astype(np.uint8).reshape(n // 512, 16, m))


K, T, S, H, N, P = 1024, 2048, 1024, 512, 1024, 512


def setup_inputs():
    n = np.random.standard_normal
    s = mx_kscale(K)[:, None]
    u = mx_kscale(H)[:, None]
    d = {}
    d["tab_words"], d["tab_scales"] = pack_weight(n((K, T)) * s, "e4m3")
    d["offs"] = striped(np.random.permutation(T)[:S])
    d["w1"] = (1.5 * n((K, H)) / K**0.5 / s).astype(np.float32)
    d["w2_words"], d["w2_scales"] = pack_weight(0.7 * n((K, H)) / K**0.5 / s, "e2m1")
    d["gain"] = (np.exp(0.3 * n(H)) * u[:, 0]).astype(np.float32)
    d["w3"] = (n((H, N)) / H**0.5 / u).astype(np.float32)
    d["base"] = (0.7 * n((N, S))).astype(np.float32)
    size = np.exp(0.8 * n(N))[None, :]
    d["w4_words"], d["w4_scales"] = pack_weight(n((H, N)) * size / H**0.5 / u, "e2m1")
    d["pos1"] = striped(np.random.permutation(S)[:P])
    d["pos2"] = striped(np.random.permutation(S)[:P])
    d["share"] = np.random.uniform(0.3, 0.9, N).astype(np.float32)
    return d


def reference(tab_words, tab_scales, offs, w1, w2_words, w2_scales, gain, w3, base,
              w4_words, w4_scales, pos1, pos2, share):
    v = unpack_weight(tab_words, tab_scales, "e4m3")[:, unstriped(offs)]
    f = mxq(f64(w1), 0, "e4m3").T @ v
    e = unpack_weight(w2_words, w2_scales, "e2m1").T @ v
    h = (f / (1.0 + np.exp(-f)) - e) * f64(gain)[:, None]
    hq = mxq(h, 0, "e4m3")
    left = (mxq(f64(w3), 0, "e4m3").T @ hq) + f64(base)
    right = unpack_weight(w4_words, w4_scales, "e2m1").T @ hq
    g2 = left * right
    y = g2[:, unstriped(pos1)] - f64(share)[:, None] * g2[:, unstriped(pos2)]
    words, scales = planes(y)
    return y, words, scales

@@ -1,0 +1,346 @@
+from contextlib import ExitStack
+
+import concourse.mybir as mybir
+
+K, T, S, H, N, PAIRS = 1024, 2048, 1024, 512, 1024, 512
+FLOPS = 2 * (2 * K * H * S + 2 * H * N * S)
+
+F32 = mybir.dt.float32
+BF16 = mybir.dt.bfloat16
+I32 = mybir.dt.int32
+U32 = mybir.dt.uint32
+U16 = mybir.dt.uint16
+U8 = mybir.dt.uint8
+FP8X4 = mybir.dt.float8_e4m3fn_x4
+FP4X4 = mybir.dt.float4_e2m1fn_x4
+ACT = mybir.ActivationFunctionType
+ALU = mybir.AluOpType
+
+P = 128
+PACK = 4
+PASS = P * PACK
+HALF = 512
+VECTOR_M = 96
+
+
+def tile_list_potline_pair_watch_kernel(
+    tc, tab_words, tab_scales, offs, w1, w2_words, w2_scales, gain, w3, base,
+    w4_words, w4_scales, pos1, pos2, share, out_0, out_1, out_2,
+):
+    nc = tc.nc
+    with ExitStack() as ctx:
+        keep = ctx.enter_context(tc.tile_pool(name="keep", bufs=1))
+        work = ctx.enter_context(tc.tile_pool(name="work", bufs=4))
+        psum_a = ctx.enter_context(tc.psum_pool(name="psum_a", bufs=4))
+        psum_b = ctx.enter_context(tc.psum_pool(name="psum_b", bufs=4))
+
+        def kept(name, shape, dtype, tag=None):
+            return keep.tile(shape, dtype, name=name, tag=tag or name, align_bytes=64)
+
+        offs_t = keep.tile([P, S // 16], U16, name="offs_t")
+        pos1_t = keep.tile([P, PAIRS // 16], U16, name="pos1_t")
+        pos2_t = keep.tile([P, PAIRS // 16], U16, name="pos2_t")
+        tab_s = kept("tab_s", [P, T], U8)
+        w2_s_raw = kept("w2_s_raw", [P, 2, PASS], U8)
+        w4_s_raw = kept("w4_s_raw", [P, 2, PASS], U8)
+        warm = kept("warm", [P, 1], F32)
+        nc.vector.memset(tab_s[:].bitcast(I32), 0)
+        nc.gpsimd.memset(w2_s_raw[:].bitcast(I32), 0)
+        nc.gpsimd.memset(w4_s_raw[:].bitcast(I32), 0)
+
+        nc.sync.dma_start(offs_t[:], offs)
+        nc.sync.dma_start(pos1_t[:], pos1)
+        nc.sync.dma_start(pos2_t[:], pos2)
+        for q in range(4):
+            nc.scalar.dma_start(
+                out=tab_s[32 * q : 32 * q + 8, :].bitcast(I32),
+                in_=tab_scales[:, 4 * q : 4 * q + 4, :].bitcast(I32),
+            )
+        tab_w = [kept(f"tab_w{a}", [P, T], U32) for a in range(2)]
+        for a in range(2):
+            nc.sync.dma_start(
+                out=tab_w[a][:].bitcast(I32),
+                in_=tab_words[a].rearrange("p t i -> p (t i)").bitcast(I32),
+            )
+        w2_w_raw = kept("w2_w_raw", [P, 2, 2 * PASS], U8)
+        nc.sync.dma_start(
+            out=w2_w_raw[:].bitcast(I32), in_=w2_words.rearrange("a p c -> p a c").bitcast(I32)
+        )
+        gain_t = kept("gain_t", [P, PACK], F32)
+        share_t = kept("share_t", [P, 2, PACK], F32)
+        for q in range(4):
+            nc.gpsimd.dma_start(
+                out=w2_s_raw[32 * q : 32 * q + 4].bitcast(I32),
+                in_=w2_scales[:, 4 * q : 4 * q + 4, :].rearrange("a r c -> r a c").bitcast(I32),
+            )
+        nc.gpsimd.dma_start(out=gain_t[:], in_=gain.rearrange("(p t) -> p t", t=PACK))
+        nc.scalar.activation(out=warm[:], in_=gain_t[:, 0:1], func=ACT.Silu)
+        for q in range(4):
+            nc.gpsimd.dma_start(
+                out=w4_s_raw[32 * q : 32 * q + 4].rearrange("r g c -> r (g c)").bitcast(I32),
+                in_=w4_scales[0, 4 * q : 4 * q + 4, :].bitcast(I32),
+            )
+        nc.gpsimd.dma_start(out=share_t[:], in_=share.rearrange("(g p t) -> p g t", g=2, t=PACK))
+
+        def load_weight(name, rows, tag):
+            raw = kept(name, [P, PACK, PASS], F32, tag=tag)
+            nc.sync.dma_start(out=raw[:], in_=rows.rearrange("(p j) c -> p j c", j=PACK))
+            return raw
+
+        base_t = []
+
+        def load_base(tag):
+            pair = len(base_t) // 2
+            g, t = divmod(2 * pair, PACK)
+            rows = base[PASS * g : PASS * (g + 1), :].rearrange("(p t) j -> p t j", t=PACK)
+            both = kept(f"base{pair}", [P, 2, S], F32, tag=tag)
+            for u in range(2):
+                nc.sync.dma_start(out=both[:, u, :], in_=rows[:, t + u, :])
+                base_t.append(both[:, u, :])
+
+        v_s0 = kept("v_s0", [P, S], U8)
+        v_s1 = kept("v_s1", [P, S], U8)
+        nc.vector.tensor_copy(out=v_s0[:], in_=tab_s[:].indirect(offs_t[:]))
+        nc.scalar.dma_start(out=v_s1[0:100, :].bitcast(I32), in_=v_s0[4:104, :].bitcast(I32))
+        v_s_fp4 = [v_s0[:], v_s1[:]]
+        v_s_fp8 = [v_s0[:], v_s0[4:128]]
+        w1_raw = [load_weight("w1_raw0", w1[0:PASS, :], "w1_raw0")]
+        v_w = [[kept(f"v_w{a}{h}", [P, HALF], U32) for h in range(2)] for a in range(2)]
+
+        def gather_words(a, h):
+            cols = offs_t[:, 32 * h : 32 * (h + 1)]
+            nc.vector.tensor_copy(out=v_w[a][h][:], in_=tab_w[a][:].indirect(cols))
+
+        def deal_fp4(name, words_raw, scales_raw):
+            words = kept(name + "_w", [P, 2, 2 * PASS], U8)
+            scales = kept(name + "_s", [P, 2, PASS], U8)
+            nc.vector.tensor_copy(
+                out=words[:].bitcast(U16).rearrange("p a (t m) -> p a t m", t=PACK),
+                in_=words_raw[:].bitcast(U16).rearrange("p a (m t) -> p a t m", t=PACK),
+            )
+            nc.vector.tensor_copy(
+                out=scales[:].rearrange("p a (t m) -> p a t m", t=PACK),
+                in_=scales_raw[:].rearrange("p a (m t) -> p a t m", t=PACK),
+            )
+            return words, scales
+
+        def round_weight(engine_copy, grouped, raw, m0, m1):
+            engine_copy(
+                out=grouped[:].rearrange("p (t m j) -> p m j t", t=PACK, j=PACK)[:, m0:m1],
+                in_=raw[:].rearrange("p j (m t) -> p m j t", t=PACK)[:, m0:m1],
+            )
+
+        def quantize(name, grouped):
+            words = kept(name + "_w", [P, PASS], U32)
+            scales = kept(name + "_s", [P, PASS], U8)
+            nc.vector.quantize_mx(out=words[:].bitcast(FP8X4), scales=scales[:], in_=grouped[:])
+            return words, scales
+
+        for h in range(2):
+            gather_words(0, h)
+        w1_raw.append(load_weight("w1_raw1", w1[PASS : 2 * PASS, :], "tab_s"))
+        for h in range(2):
+            gather_words(1, h)
+        w3_raw = [load_weight("w3_raw0", w3[:, 0:PASS], "tab_w0")]
+        w2_w, w2_s = deal_fp4("w2", w2_w_raw, w2_s_raw)
+        w4_w_raw = kept("w4_w_raw", [P, 2, 2 * PASS], U8, tag="w2_w_raw")
+        nc.sync.dma_start(
+            out=w4_w_raw[:].rearrange("p g c -> p (g c)").bitcast(I32), in_=w4_words[0].bitcast(I32)
+        )
+
+        w1_bf = [kept(f"w1_bf{a}", [P, PACK * H], BF16) for a in range(2)]
+        round_weight(nc.scalar.copy, w1_bf[0], w1_raw[0], 0, P)
+        load_base("tab_w1")
+        load_base("w1_raw0")
+        w1_q = [quantize("w1q0", w1_bf[0])]
+        round_weight(nc.vector.tensor_copy, w1_bf[1], w1_raw[1], 0, VECTOR_M)
+        round_weight(nc.scalar.copy, w1_bf[1], w1_raw[1], VECTOR_M, P)
+        load_base("tab_s")
+        w1_q.append(quantize("w1q1", w1_bf[1]))
+
+        def first_products(h):
+            e_ps, f_ps = [], []
+            for t in range(PACK):
+                acc = psum_a.tile([P, HALF], F32, name="acc_a")
+                for a in range(2):
+                    nc.tensor.matmul_mx(
+                        out=acc[:],
+                        lhsT=w2_w[:, a, 2 * P * t : 2 * P * (t + 1)].bitcast(FP4X4),
+                        lhsT_scale=w2_s[:, a, P * t : P * (t + 1)],
+                        rhs=v_w[a][h][:].bitcast(FP8X4),
+                        rhs_scale=v_s_fp4[a][:, HALF * h : HALF * (h + 1)],
+                        start=(a == 0), stop=(a == 1),
+                    )
+                e_ps.append(acc)
+            f_ps = [psum_b.tile([P, HALF], F32, name="acc_b") for t in range(PACK)]
+            for a in range(2):
+                for t in range(PACK):
+                    nc.tensor.matmul_mx(
+                        out=f_ps[t][:],
+                        lhsT=w1_q[a][0][:, P * t : P * (t + 1)].bitcast(FP8X4),
+                        lhsT_scale=w1_q[a][1][:, P * t : P * (t + 1)],
+                        rhs=v_w[a][h][:].bitcast(FP8X4),
+                        rhs_scale=v_s_fp8[a][:, HALF * h : HALF * (h + 1)],
+                        start=(a == 0), stop=(a == 1),
+                    )
+            return e_ps, f_ps
+
+        def walk(ap, pattern):
+            return ap.rearrange(pattern + " -> p c t i", t=PACK, i=4)
+
+        h_bf = [kept(f"h_bf{h}", [P, HALF * PACK], BF16) for h in range(2)]
+
+        e_ps, f_ps = first_products(0)
+        w3_raw.append(load_weight("w3_raw1", w3[:, PASS : 2 * PASS], "v_w00"))
+        diff = kept("diff", [P, PACK, HALF], F32)
+        for t in range(PACK):
+            act = work.tile([P, HALF], F32, name="act")
+            nc.scalar.activation(out=act[:], in_=f_ps[t][:], func=ACT.Silu)
+            nc.vector.tensor_tensor(out=diff[:, t, :], in0=act[:], in1=e_ps[t][:], op=ALU.subtract)
+        nc.vector.tensor_tensor(
+            out=walk(h_bf[0][:], "p (c i t)"),
+            in0=walk(diff[:], "p t (c i)"),
+            in1=gain_t[:].unsqueeze(1).unsqueeze(3).to_broadcast([P, HALF // 4, PACK, 4]),
+            op=ALU.mult,
+        )
+        w3_bf = [kept(f"w3_bf{g}", [P, PACK * PASS], BF16) for g in range(2)]
+        round_weight(nc.scalar.copy, w3_bf[0], w3_raw[0], 0, P)
+        load_base("tab_w0")
+        w4_w, w4_s = deal_fp4("w4", w4_w_raw, w4_s_raw)
+        h_q = [quantize("hq0", h_bf[0])]
+        w3_q = [quantize("w3q0", w3_bf[0])]
+
+        e_ps, f_ps = first_products(1)
+        h_rows = kept("h_rows", [P, PACK, HALF], BF16)
+        for t in range(PACK):
+            eg = work.tile([P, HALF], F32, name="eg")
+            nc.scalar.activation(out=eg[:], in_=e_ps[t][:], func=ACT.Copy, scale=gain_t[:, t : t + 1])
+            act = work.tile([P, HALF], F32, name="act")
+            nc.scalar.activation(out=act[:], in_=f_ps[t][:], func=ACT.Silu)
+            nc.vector.scalar_tensor_tensor(
+                out=h_rows[:, t, :], in0=act[:], scalar=gain_t[:, t : t + 1], in1=eg[:],
+                op0=ALU.mult, op1=ALU.subtract,
+            )
+        nc.scalar.copy(out=walk(h_bf[1][:], "p (c i t)"), in_=walk(h_rows[:], "p t (c i)"))
+
+        g2 = [kept(f"g2_{i}", [P, S], F32) for i in range(8)]
+
+        def second_products(i, h):
+            g, t = divmod(i, PACK)
+            left = psum_b.tile([P, HALF], F32, name="acc_b")
+            right = psum_a.tile([P, HALF], F32, name="acc_a")
+            nc.tensor.matmul_mx(
+                out=left[:],
+                lhsT=w3_q[g][0][:, P * t : P * (t + 1)].bitcast(FP8X4),
+                lhsT_scale=w3_q[g][1][:, P * t : P * (t + 1)],
+                rhs=h_q[h][0][:].bitcast(FP8X4), rhs_scale=h_q[h][1][:],
+                start=True, stop=True,
+            )
+            nc.tensor.matmul_mx(
+                out=right[:],
+                lhsT=w4_w[:, g, 2 * P * t : 2 * P * (t + 1)].bitcast(FP4X4),
+                lhsT_scale=w4_s[:, g, P * t : P * (t + 1)],
+                rhs=h_q[h][0][:].bitcast(FP8X4), rhs_scale=h_q[h][1][:],
+                start=True, stop=True,
+            )
+            return left, right
+
+        def combine(units):
+            banks = [second_products(i, h) for i, h in units]
+            sums = []
+            for (i, h), (left, right) in zip(units, banks):
+                total = work.tile([P, HALF], F32, name="total")
+                nc.vector.tensor_tensor(
+                    out=total[:], in0=left[:], in1=base_t[i][:, HALF * h : HALF * (h + 1)], op=ALU.add
+                )
+                sums.append(total)
+            for (i, h), (left, right), total in zip(units, banks, sums):
+                nc.vector.tensor_tensor(
+                    out=g2[i][:, HALF * h : HALF * (h + 1)], in0=right[:], in1=total[:], op=ALU.mult
+                )
+
+        y = [kept(f"y{g}", [P, PACK, PAIRS], F32) for g in range(2)]
+        y_bf = [kept(f"y_bf{g}", [P, PAIRS * PACK], BF16, tag=f"w1_bf{g}") for g in range(2)]
+        y_w = [kept(f"y_w{g}", [P, PAIRS], U32) for g in range(2)]
+        y_s = [kept(f"y_s{g}", [P, PAIRS], U8) for g in range(2)]
+        scaled = {}
+
+        def pick_paired(i, m0=0, m1=PAIRS):
+            g, t = divmod(i, PACK)
+            paired = work.tile([P, m1 - m0], F32, name="paired")
+            nc.vector.tensor_copy(out=paired[:], in_=g2[i][:].indirect(pos2_t[:, m0 // 16 : m1 // 16]))
+            scaled[i, m0] = work.tile([P, m1 - m0], F32, name="scaled")
+            nc.scalar.activation(
+                out=scaled[i, m0][:], in_=paired[:], func=ACT.Copy, scale=share_t[:, g, t : t + 1]
+            )
+
+        def pick_first(i, m0=0, m1=PAIRS):
+            g, t = divmod(i, PACK)
+            nc.vector.tensor_tensor(
+                out=y[g][:, t, m0:m1], in0=g2[i][:].indirect(pos1_t[:, m0 // 16 : m1 // 16]),
+                in1=scaled[i, m0][:], op=ALU.subtract,
+            )
+            rows = out_0[PASS * g : PASS * (g + 1), :].rearrange("(p t) m -> p t m", t=PACK)
+            nc.sync.dma_start(out=rows[:, t, m0:m1], in_=y[g][:, t, m0:m1])
+
+        def round_y(g, engine_copy, m0, m1):
+            engine_copy(
+                out=walk(y_bf[g][:, PACK * m0 : PACK * m1], "p (c i t)"),
+                in_=walk(y[g][:, :, m0:m1], "p t (c i)"),
+            )
+
+        def quantize_y(g, m0, m1):
+            nc.vector.quantize_mx(
+                out=y_w[g][:, m0:m1].bitcast(FP8X4), scales=y_s[g][:, m0:m1],
+                in_=y_bf[g][:, PACK * m0 : PACK * m1],
+            )
+            words = out_1[g].rearrange("p m t -> p (m t)").bitcast(I32)
+            nc.sync.dma_start(out=words[:, m0:m1], in_=y_w[g][:, m0:m1].bitcast(I32))
+
+        def store_scales(g):
+            for q in range(4):
+                queue = nc.scalar if q % 2 else nc.sync
+                queue.dma_start(
+                    out=out_2[g, 4 * q : 4 * q + 4, :].bitcast(I32),
+                    in_=y_s[g][32 * q : 32 * q + 4, :].bitcast(I32),
+                )
+
+        combine([(0, 0), (1, 0)])
+        combine([(2, 0), (3, 0)])
+        h_q.append(quantize("hq1", h_bf[1]))
+        round_weight(nc.scalar.copy, w3_bf[1], w3_raw[1], 0, P)
+        combine([(0, 1), (1, 1)])
+        pick_paired(0)
+        pick_paired(1)
+        w3_q.append(quantize("w3q1", w3_bf[1]))
+        combine([(2, 1), (3, 1)])
+        pick_first(0)
+        pick_paired(2)
+        pick_first(1)
+        pick_paired(3)
+        combine([(4, 0), (4, 1)])
+        pick_first(2)
+        pick_first(3)
+        pick_paired(4)
+        mid = PAIRS // 2
+        round_y(0, nc.scalar.copy, 0, mid)
+        combine([(5, 0), (5, 1)])
+        pick_first(4)
+        pick_paired(5)
+        round_y(0, nc.scalar.copy, mid, PAIRS)
+        combine([(6, 0), (6, 1)])
+        pick_first(5)
+        pick_paired(6)
+        quantize_y(0, 0, PAIRS)
+        store_scales(0)
+        combine([(7, 0), (7, 1)])
+        pick_first(6)
+        pick_paired(7, 0, mid)
+        pick_paired(7, mid, PAIRS)
+        pick_first(7, 0, mid)
+        round_y(1, nc.scalar.copy, 0, mid)
+        pick_first(7, mid, PAIRS)
+        round_y(1, nc.vector.tensor_copy, mid, PAIRS)
+        quantize_y(1, 0, mid)
+        quantize_y(1, mid, PAIRS)
+        store_scales(1)

@@ -20,6 +20,7 @@ P = 128
 PACK = 4
 PASS = P * PACK
 HALF = 512
+BANK = 2048
 VECTOR_M = 96
 
 
@@ -30,11 +31,14 @@ def tile_list_potline_pair_watch_kernel(
     nc = tc.nc
     with ExitStack() as ctx:
         keep = ctx.enter_context(tc.tile_pool(name="keep", bufs=1))
+        staged = ctx.enter_context(tc.tile_pool(name="staged", bufs=1))
         work = ctx.enter_context(tc.tile_pool(name="work", bufs=4))
-        psum_a = ctx.enter_context(tc.psum_pool(name="psum_a", bufs=4))
+        psum_a = ctx.enter_context(tc.psum_pool(name="psum_a", bufs=1))
         psum_b = ctx.enter_context(tc.psum_pool(name="psum_b", bufs=4))
 
         def kept(name, shape, dtype, tag=None):
+            if isinstance(tag, int):
+                return staged.tile(shape, dtype, name=name, align_bytes=64, offset=tag)
             return keep.tile(shape, dtype, name=name, tag=tag or name, align_bytes=64)
 
         offs_t = keep.tile([P, S // 16], U16, name="offs_t")
@@ -43,10 +47,12 @@ def tile_list_potline_pair_watch_kernel(
         tab_s = kept("tab_s", [P, T], U8)
         w2_s_raw = kept("w2_s_raw", [P, 2, PASS], U8)
         w4_s_raw = kept("w4_s_raw", [P, 2, PASS], U8)
-        warm = kept("warm", [P, 1], F32)
+        warm_in = kept("warm_in", [P, 1], F32)
+        warm_out = kept("warm_out", [P, 1], F32)
         nc.vector.memset(tab_s[:].bitcast(I32), 0)
         nc.gpsimd.memset(w2_s_raw[:].bitcast(I32), 0)
         nc.gpsimd.memset(w4_s_raw[:].bitcast(I32), 0)
+        nc.vector.memset(warm_in[:], 0.0)
 
         nc.sync.dma_start(offs_t[:], offs)
         nc.sync.dma_start(pos1_t[:], pos1)
@@ -56,7 +62,8 @@ def tile_list_potline_pair_watch_kernel(
                 out=tab_s[32 * q : 32 * q + 8, :].bitcast(I32),
                 in_=tab_scales[:, 4 * q : 4 * q + 4, :].bitcast(I32),
             )
-        tab_w = [kept(f"tab_w{a}", [P, T], U32) for a in range(2)]
+        nc.scalar.activation(out=warm_out[:], in_=warm_in[:], func=ACT.Silu)
+        tab_w = [kept("tab_w0", [P, T], U32, tag=1024), kept("tab_w1", [P, T], U32)]
         for a in range(2):
             nc.sync.dma_start(
                 out=tab_w[a][:].bitcast(I32),
@@ -66,21 +73,16 @@ def tile_list_potline_pair_watch_kernel(
         nc.sync.dma_start(
             out=w2_w_raw[:].bitcast(I32), in_=w2_words.rearrange("a p c -> p a c").bitcast(I32)
         )
-        gain_t = kept("gain_t", [P, PACK], F32)
-        share_t = kept("share_t", [P, 2, PACK], F32)
         for q in range(4):
             nc.gpsimd.dma_start(
                 out=w2_s_raw[32 * q : 32 * q + 4].bitcast(I32),
                 in_=w2_scales[:, 4 * q : 4 * q + 4, :].rearrange("a r c -> r a c").bitcast(I32),
             )
-        nc.gpsimd.dma_start(out=gain_t[:], in_=gain.rearrange("(p t) -> p t", t=PACK))
-        nc.scalar.activation(out=warm[:], in_=gain_t[:, 0:1], func=ACT.Silu)
         for q in range(4):
             nc.gpsimd.dma_start(
                 out=w4_s_raw[32 * q : 32 * q + 4].rearrange("r g c -> r (g c)").bitcast(I32),
                 in_=w4_scales[0, 4 * q : 4 * q + 4, :].bitcast(I32),
             )
-        nc.gpsimd.dma_start(out=share_t[:], in_=share.rearrange("(g p t) -> p g t", g=2, t=PACK))
 
         def load_weight(name, rows, tag):
             raw = kept(name, [P, PACK, PASS], F32, tag=tag)
@@ -101,19 +103,20 @@ def tile_list_potline_pair_watch_kernel(
         v_s0 = kept("v_s0", [P, S], U8)
         v_s1 = kept("v_s1", [P, S], U8)
         nc.vector.tensor_copy(out=v_s0[:], in_=tab_s[:].indirect(offs_t[:]))
-        nc.scalar.dma_start(out=v_s1[0:100, :].bitcast(I32), in_=v_s0[4:104, :].bitcast(I32))
+        nc.sync.dma_start(out=v_s1[0:100, :].bitcast(I32), in_=v_s0[4:104, :].bitcast(I32))
         v_s_fp4 = [v_s0[:], v_s1[:]]
         v_s_fp8 = [v_s0[:], v_s0[4:128]]
         w1_raw = [load_weight("w1_raw0", w1[0:PASS, :], "w1_raw0")]
-        v_w = [[kept(f"v_w{a}{h}", [P, HALF], U32) for h in range(2)] for a in range(2)]
+        v_w = {}
 
-        def gather_words(a, h):
+        def gather_words(a, h, tag=None):
+            v_w[a, h] = kept(f"v_w{a}{h}", [P, HALF], U32, tag=tag)
             cols = offs_t[:, 32 * h : 32 * (h + 1)]
-            nc.vector.tensor_copy(out=v_w[a][h][:], in_=tab_w[a][:].indirect(cols))
+            nc.vector.tensor_copy(out=v_w[a, h][:], in_=tab_w[a][:].indirect(cols))
 
-        def deal_fp4(name, words_raw, scales_raw):
+        def deal_fp4(name, words_raw, scales_raw, tag):
             words = kept(name + "_w", [P, 2, 2 * PASS], U8)
-            scales = kept(name + "_s", [P, 2, PASS], U8)
+            scales = kept(name + "_s", [P, 2, PASS], U8, tag=tag)
             nc.vector.tensor_copy(
                 out=words[:].bitcast(U16).rearrange("p a (t m) -> p a t m", t=PACK),
                 in_=words_raw[:].bitcast(U16).rearrange("p a (m t) -> p a t m", t=PACK),
@@ -136,13 +139,14 @@ def tile_list_potline_pair_watch_kernel(
             nc.vector.quantize_mx(out=words[:].bitcast(FP8X4), scales=scales[:], in_=grouped[:])
             return words, scales
 
-        for h in range(2):
-            gather_words(0, h)
         w1_raw.append(load_weight("w1_raw1", w1[PASS : 2 * PASS, :], "tab_s"))
-        for h in range(2):
-            gather_words(1, h)
-        w3_raw = [load_weight("w3_raw0", w3[:, 0:PASS], "tab_w0")]
-        w2_w, w2_s = deal_fp4("w2", w2_w_raw, w2_s_raw)
+        gather_words(0, 0)
+        gather_words(0, 1)
+        w3_raw = [load_weight("w3_raw0", w3[:, 0:PASS], 0)]
+        gather_words(1, 0)
+        w2_w, w2_s = deal_fp4("w2", w2_w_raw, w2_s_raw, 8192)
+        gain_t = kept("gain_t", [P, PACK], F32, tag="w2_s_raw")
+        nc.sync.dma_start(out=gain_t[:], in_=gain.rearrange("(p t) -> p t", t=PACK))
         w4_w_raw = kept("w4_w_raw", [P, 2, 2 * PASS], U8, tag="w2_w_raw")
         nc.sync.dma_start(
             out=w4_w_raw[:].rearrange("p g c -> p (g c)").bitcast(I32), in_=w4_words[0].bitcast(I32)
@@ -150,36 +154,41 @@ def tile_list_potline_pair_watch_kernel(
 
         w1_bf = [kept(f"w1_bf{a}", [P, PACK * H], BF16) for a in range(2)]
         round_weight(nc.scalar.copy, w1_bf[0], w1_raw[0], 0, P)
-        load_base("tab_w1")
         load_base("w1_raw0")
         w1_q = [quantize("w1q0", w1_bf[0])]
         round_weight(nc.vector.tensor_copy, w1_bf[1], w1_raw[1], 0, VECTOR_M)
         round_weight(nc.scalar.copy, w1_bf[1], w1_raw[1], VECTOR_M, P)
-        load_base("tab_s")
         w1_q.append(quantize("w1q1", w1_bf[1]))
+        gather_words(1, 1, tag="tab_s")
+        share_t = kept("share_t", [P, 2, PACK], F32, tag="w1_bf1")
+        nc.sync.dma_start(out=share_t[:], in_=share.rearrange("(g p t) -> p g t", g=2, t=PACK))
+        load_base("tab_w1")
 
         def first_products(h):
             e_ps, f_ps = [], []
+            e_all = psum_a.tile([P, PACK, HALF], F32, name="e1", offset=0) if h else None
             for t in range(PACK):
-                acc = psum_a.tile([P, HALF], F32, name="acc_a")
+                acc = e_all[:, t, :] if h else psum_a.tile([P, HALF], F32, name=f"e0{t}", offset=BANK * t)[:]
                 for a in range(2):
                     nc.tensor.matmul_mx(
-                        out=acc[:],
+                        out=acc,
                         lhsT=w2_w[:, a, 2 * P * t : 2 * P * (t + 1)].bitcast(FP4X4),
                         lhsT_scale=w2_s[:, a, P * t : P * (t + 1)],
-                        rhs=v_w[a][h][:].bitcast(FP8X4),
+                        rhs=v_w[a, h][:].bitcast(FP8X4),
                         rhs_scale=v_s_fp4[a][:, HALF * h : HALF * (h + 1)],
                         start=(a == 0), stop=(a == 1),
                     )
                 e_ps.append(acc)
-            f_ps = [psum_b.tile([P, HALF], F32, name="acc_b") for t in range(PACK)]
-            for a in range(2):
-                for t in range(PACK):
+            steps = [(a, t) for t in range(PACK) for a in range(2)]
+            for a, t in sorted(steps) if h == 0 else steps:
+                if a == 0:
+                    f_ps.append(psum_b.tile([P, HALF], F32, name="acc_b"))
+                if True:
                     nc.tensor.matmul_mx(
                         out=f_ps[t][:],
                         lhsT=w1_q[a][0][:, P * t : P * (t + 1)].bitcast(FP8X4),
                         lhsT_scale=w1_q[a][1][:, P * t : P * (t + 1)],
-                        rhs=v_w[a][h][:].bitcast(FP8X4),
+                        rhs=v_w[a, h][:].bitcast(FP8X4),
                         rhs_scale=v_s_fp8[a][:, HALF * h : HALF * (h + 1)],
                         start=(a == 0), stop=(a == 1),
                     )
@@ -190,45 +199,56 @@ def tile_list_potline_pair_watch_kernel(
 
         h_bf = [kept(f"h_bf{h}", [P, HALF * PACK], BF16) for h in range(2)]
 
-        e_ps, f_ps = first_products(0)
+        def features(h):
+            e_ps, f_ps = first_products(h)
+            diff = kept(f"diff{h}", [P, PACK, HALF], F32, tag="diff")
+            for t in range(PACK):
+                act = work.tile([P, HALF], F32, name="act")
+                nc.scalar.activation(out=act[:], in_=f_ps[t][:], func=ACT.Silu)
+                nc.vector.tensor_tensor(out=diff[:, t, :], in0=act[:], in1=e_ps[t], op=ALU.subtract)
+            nc.vector.tensor_tensor(
+                out=walk(h_bf[h][:], "p (c i t)"),
+                in0=walk(diff[:], "p t (c i)"),
+                in1=gain_t[:].unsqueeze(1).unsqueeze(3).to_broadcast([P, HALF // 4, PACK, 4]),
+                op=ALU.mult,
+            )
+
+        features(0)
         w3_raw.append(load_weight("w3_raw1", w3[:, PASS : 2 * PASS], "v_w00"))
-        diff = kept("diff", [P, PACK, HALF], F32)
-        for t in range(PACK):
-            act = work.tile([P, HALF], F32, name="act")
-            nc.scalar.activation(out=act[:], in_=f_ps[t][:], func=ACT.Silu)
-            nc.vector.tensor_tensor(out=diff[:, t, :], in0=act[:], in1=e_ps[t][:], op=ALU.subtract)
-        nc.vector.tensor_tensor(
-            out=walk(h_bf[0][:], "p (c i t)"),
-            in0=walk(diff[:], "p t (c i)"),
-            in1=gain_t[:].unsqueeze(1).unsqueeze(3).to_broadcast([P, HALF // 4, PACK, 4]),
-            op=ALU.mult,
-        )
         w3_bf = [kept(f"w3_bf{g}", [P, PACK * PASS], BF16) for g in range(2)]
-        round_weight(nc.scalar.copy, w3_bf[0], w3_raw[0], 0, P)
-        load_base("tab_w0")
-        w4_w, w4_s = deal_fp4("w4", w4_w_raw, w4_s_raw)
+        round_weight(nc.scalar.copy, w3_bf[0], w3_raw[0], 0, P // 2)
+        round_weight(nc.scalar.copy, w3_bf[0], w3_raw[0], P // 2, P)
+        load_base(0)
         h_q = [quantize("hq0", h_bf[0])]
         w3_q = [quantize("w3q0", w3_bf[0])]
-
-        e_ps, f_ps = first_products(1)
-        h_rows = kept("h_rows", [P, PACK, HALF], BF16)
-        for t in range(PACK):
-            eg = work.tile([P, HALF], F32, name="eg")
-            nc.scalar.activation(out=eg[:], in_=e_ps[t][:], func=ACT.Copy, scale=gain_t[:, t : t + 1])
-            act = work.tile([P, HALF], F32, name="act")
-            nc.scalar.activation(out=act[:], in_=f_ps[t][:], func=ACT.Silu)
-            nc.vector.scalar_tensor_tensor(
-                out=h_rows[:, t, :], in0=act[:], scalar=gain_t[:, t : t + 1], in1=eg[:],
-                op0=ALU.mult, op1=ALU.subtract,
-            )
-        nc.scalar.copy(out=walk(h_bf[1][:], "p (c i t)"), in_=walk(h_rows[:], "p t (c i)"))
+        w4_w, w4_s = deal_fp4("w4", w4_w_raw, w4_s_raw, "v_w10")
 
         g2 = [kept(f"g2_{i}", [P, S], F32) for i in range(8)]
 
-        def second_products(i, h):
+        def offset_left(i, halves):
             g, t = divmod(i, PACK)
+            cols = slice(HALF * halves[0], HALF * (halves[-1] + 1))
+            left_sb = work.tile([P, S], F32, name="left_sb")
+            for h in halves:
+                left = psum_b.tile([P, HALF], F32, name="acc_b")
+                nc.tensor.matmul_mx(
+                    out=left[:],
+                    lhsT=w3_q[g][0][:, P * t : P * (t + 1)].bitcast(FP8X4),
+                    lhsT_scale=w3_q[g][1][:, P * t : P * (t + 1)],
+                    rhs=h_q[h][0][:].bitcast(FP8X4), rhs_scale=h_q[h][1][:],
+                    start=True, stop=True,
+                )
+                nc.scalar.copy(out=left_sb[:, HALF * h : HALF * (h + 1)], in_=left[:])
+            nc.gpsimd.tensor_tensor(
+                out=g2[i][:, cols], in0=left_sb[:, cols], in1=base_t[i][:, cols], op=ALU.add
+            )
+
+        rights = []
+
+        def offset_left_on_vector(i, h):
+            g, t = divmod(i, PACK)
+            cols = slice(HALF * h, HALF * (h + 1))
             left = psum_b.tile([P, HALF], F32, name="acc_b")
-            right = psum_a.tile([P, HALF], F32, name="acc_a")
             nc.tensor.matmul_mx(
                 out=left[:],
                 lhsT=w3_q[g][0][:, P * t : P * (t + 1)].bitcast(FP8X4),
@@ -236,40 +256,34 @@ def tile_list_potline_pair_watch_kernel(
                 rhs=h_q[h][0][:].bitcast(FP8X4), rhs_scale=h_q[h][1][:],
                 start=True, stop=True,
             )
-            nc.tensor.matmul_mx(
-                out=right[:],
-                lhsT=w4_w[:, g, 2 * P * t : 2 * P * (t + 1)].bitcast(FP4X4),
-                lhsT_scale=w4_s[:, g, P * t : P * (t + 1)],
-                rhs=h_q[h][0][:].bitcast(FP8X4), rhs_scale=h_q[h][1][:],
-                start=True, stop=True,
-            )
-            return left, right
+            nc.vector.tensor_tensor(out=g2[i][:, cols], in0=left[:], in1=base_t[i][:, cols], op=ALU.add)
 
-        def combine(units):
-            banks = [second_products(i, h) for i, h in units]
-            sums = []
-            for (i, h), (left, right) in zip(units, banks):
-                total = work.tile([P, HALF], F32, name="total")
-                nc.vector.tensor_tensor(
-                    out=total[:], in0=left[:], in1=base_t[i][:, HALF * h : HALF * (h + 1)], op=ALU.add
+        def times_right(i, halves):
+            g, t = divmod(i, PACK)
+            for h in halves:
+                right = psum_a.tile([P, HALF], F32, name=f"right{i}{h}", offset=BANK * (len(rights) % PACK))
+                rights.append(right)
+                nc.tensor.matmul_mx(
+                    out=right[:],
+                    lhsT=w4_w[:, g, 2 * P * t : 2 * P * (t + 1)].bitcast(FP4X4),
+                    lhsT_scale=w4_s[:, g, P * t : P * (t + 1)],
+                    rhs=h_q[h][0][:].bitcast(FP8X4), rhs_scale=h_q[h][1][:],
+                    start=True, stop=True,
                 )
-                sums.append(total)
-            for (i, h), (left, right), total in zip(units, banks, sums):
-                nc.vector.tensor_tensor(
-                    out=g2[i][:, HALF * h : HALF * (h + 1)], in0=right[:], in1=total[:], op=ALU.mult
-                )
+                part = g2[i][:, HALF * h : HALF * (h + 1)]
+                nc.vector.tensor_tensor(out=part, in0=right[:], in1=part, op=ALU.mult)
 
         y = [kept(f"y{g}", [P, PACK, PAIRS], F32) for g in range(2)]
-        y_bf = [kept(f"y_bf{g}", [P, PAIRS * PACK], BF16, tag=f"w1_bf{g}") for g in range(2)]
+        y_bf = [kept(f"y_bf{g}", [P, PAIRS * PACK], BF16) for g in range(2)]
         y_w = [kept(f"y_w{g}", [P, PAIRS], U32) for g in range(2)]
         y_s = [kept(f"y_s{g}", [P, PAIRS], U8) for g in range(2)]
         scaled = {}
 
         def pick_paired(i, m0=0, m1=PAIRS):
             g, t = divmod(i, PACK)
-            paired = work.tile([P, m1 - m0], F32, name="paired")
+            paired = work.tile([P, m1 - m0], F32, name="paired", bufs=3)
             nc.vector.tensor_copy(out=paired[:], in_=g2[i][:].indirect(pos2_t[:, m0 // 16 : m1 // 16]))
-            scaled[i, m0] = work.tile([P, m1 - m0], F32, name="scaled")
+            scaled[i, m0] = work.tile([P, m1 - m0], F32, name="scaled", bufs=3)
             nc.scalar.activation(
                 out=scaled[i, m0][:], in_=paired[:], func=ACT.Copy, scale=share_t[:, g, t : t + 1]
             )
@@ -282,6 +296,17 @@ def tile_list_potline_pair_watch_kernel(
             )
             rows = out_0[PASS * g : PASS * (g + 1), :].rearrange("(p t) m -> p t m", t=PACK)
             nc.sync.dma_start(out=rows[:, t, m0:m1], in_=y[g][:, t, m0:m1])
+
+        def pick_both(i):
+            g, t = divmod(i, PACK)
+            pick_paired(i)
+            first = work.tile([P, PAIRS], F32, name="first", bufs=3)
+            nc.vector.tensor_copy(out=first[:], in_=g2[i][:].indirect(pos1_t[:]))
+            nc.gpsimd.tensor_tensor(
+                out=y[g][:, t, :], in0=first[:], in1=scaled[i, 0][:], op=ALU.subtract
+            )
+            rows = out_0[PASS * g : PASS * (g + 1), :].rearrange("(p t) m -> p t m", t=PACK)
+            nc.sync.dma_start(out=rows[:, t, :], in_=y[g][:, t, :])
 
         def round_y(g, engine_copy, m0, m1):
             engine_copy(
@@ -305,36 +330,32 @@ def tile_list_potline_pair_watch_kernel(
                     in_=y_s[g][32 * q : 32 * q + 4, :].bitcast(I32),
                 )
 
-        combine([(0, 0), (1, 0)])
-        combine([(2, 0), (3, 0)])
-        h_q.append(quantize("hq1", h_bf[1]))
-        round_weight(nc.scalar.copy, w3_bf[1], w3_raw[1], 0, P)
-        combine([(0, 1), (1, 1)])
-        pick_paired(0)
-        pick_paired(1)
-        w3_q.append(quantize("w3q1", w3_bf[1]))
-        combine([(2, 1), (3, 1)])
-        pick_first(0)
-        pick_paired(2)
-        pick_first(1)
-        pick_paired(3)
-        combine([(4, 0), (4, 1)])
-        pick_first(2)
-        pick_first(3)
-        pick_paired(4)
         mid = PAIRS // 2
-        round_y(0, nc.scalar.copy, 0, mid)
-        combine([(5, 0), (5, 1)])
-        pick_first(4)
-        pick_paired(5)
-        round_y(0, nc.scalar.copy, mid, PAIRS)
-        combine([(6, 0), (6, 1)])
-        pick_first(5)
-        pick_paired(6)
-        quantize_y(0, 0, PAIRS)
-        store_scales(0)
-        combine([(7, 0), (7, 1)])
-        pick_first(6)
+        for i in range(PACK):
+            offset_left(i, [0])
+        features(1)
+        load_base("tab_s")
+        h_q.append(quantize("hq1", h_bf[1]))
+        offset_left_on_vector(0, 1)
+        for i in range(PACK):
+            times_right(i, [0])
+        offset_left(1, [1])
+        round_weight(nc.scalar.copy, w3_bf[1], w3_raw[1], 0, P // 2)
+        round_weight(nc.scalar.copy, w3_bf[1], w3_raw[1], P // 2, P)
+        w3_q.append(quantize("w3q1", w3_bf[1]))
+        for i in range(8):
+            if i + 2 < 8:
+                offset_left(i + 2, [1] if i + 2 < PACK else [0, 1])
+            times_right(i, [1] if i < PACK else [0, 1])
+            if i < 7:
+                pick_both(i)
+            if i == 4:
+                round_y(0, nc.scalar.copy, 0, mid)
+            if i == 5:
+                round_y(0, nc.scalar.copy, mid, PAIRS)
+            if i == 6:
+                quantize_y(0, 0, PAIRS)
+                store_scales(0)
         pick_paired(7, 0, mid)
         pick_paired(7, mid, PAIRS)
         pick_first(7, 0, mid)

@@ -33,7 +33,7 @@ def tile_list_potline_pair_watch_kernel(
         keep = ctx.enter_context(tc.tile_pool(name="keep", bufs=1))
         staged = ctx.enter_context(tc.tile_pool(name="staged", bufs=1))
         work = ctx.enter_context(tc.tile_pool(name="work", bufs=4))
-        psum_a = ctx.enter_context(tc.psum_pool(name="psum_a", bufs=1))
+        psum_a = ctx.enter_context(tc.psum_pool(name="psum_a", bufs=4))
         psum_b = ctx.enter_context(tc.psum_pool(name="psum_b", bufs=4))
 
         def kept(name, shape, dtype, tag=None):
@@ -46,12 +46,10 @@ def tile_list_potline_pair_watch_kernel(
         pos2_t = keep.tile([P, PAIRS // 16], U16, name="pos2_t")
         tab_s = kept("tab_s", [P, T], U8)
         w2_s_raw = kept("w2_s_raw", [P, 2, PASS], U8)
-        w4_s_raw = kept("w4_s_raw", [P, 2, PASS], U8)
         warm_in = kept("warm_in", [P, 1], F32)
         warm_out = kept("warm_out", [P, 1], F32)
         nc.vector.memset(tab_s[:].bitcast(I32), 0)
         nc.gpsimd.memset(w2_s_raw[:].bitcast(I32), 0)
-        nc.gpsimd.memset(w4_s_raw[:].bitcast(I32), 0)
         nc.vector.memset(warm_in[:], 0.0)
 
         nc.sync.dma_start(offs_t[:], offs)
@@ -78,11 +76,8 @@ def tile_list_potline_pair_watch_kernel(
                 out=w2_s_raw[32 * q : 32 * q + 4].bitcast(I32),
                 in_=w2_scales[:, 4 * q : 4 * q + 4, :].rearrange("a r c -> r a c").bitcast(I32),
             )
-        for q in range(4):
-            nc.gpsimd.dma_start(
-                out=w4_s_raw[32 * q : 32 * q + 4].rearrange("r g c -> r (g c)").bitcast(I32),
-                in_=w4_scales[0, 4 * q : 4 * q + 4, :].bitcast(I32),
-            )
+        gain_t = kept("gain_t", [P, PACK], F32, tag="warm_in")
+        nc.sync.dma_start(out=gain_t[:], in_=gain.rearrange("(p t) -> p t", t=PACK))
 
         def load_weight(name, rows, tag):
             raw = kept(name, [P, PACK, PASS], F32, tag=tag)
@@ -145,16 +140,18 @@ def tile_list_potline_pair_watch_kernel(
         w3_raw = [load_weight("w3_raw0", w3[:, 0:PASS], 0)]
         gather_words(1, 0)
         w2_w, w2_s = deal_fp4("w2", w2_w_raw, w2_s_raw, 8192)
-        gain_t = kept("gain_t", [P, PACK], F32, tag="w2_s_raw")
-        nc.sync.dma_start(out=gain_t[:], in_=gain.rearrange("(p t) -> p t", t=PACK))
         w4_w_raw = kept("w4_w_raw", [P, 2, 2 * PASS], U8, tag="w2_w_raw")
         nc.sync.dma_start(
             out=w4_w_raw[:].rearrange("p g c -> p (g c)").bitcast(I32), in_=w4_words[0].bitcast(I32)
         )
+        for q in range(4):
+            nc.sync.dma_start(
+                out=w2_s_raw[32 * q : 32 * q + 4].rearrange("r g c -> r (g c)").bitcast(I32),
+                in_=w4_scales[0, 4 * q : 4 * q + 4, :].bitcast(I32),
+            )
 
         w1_bf = [kept(f"w1_bf{a}", [P, PACK * H], BF16) for a in range(2)]
         round_weight(nc.scalar.copy, w1_bf[0], w1_raw[0], 0, P)
-        load_base("w1_raw0")
         w1_q = [quantize("w1q0", w1_bf[0])]
         round_weight(nc.vector.tensor_copy, w1_bf[1], w1_raw[1], 0, VECTOR_M)
         round_weight(nc.scalar.copy, w1_bf[1], w1_raw[1], VECTOR_M, P)
@@ -166,9 +163,8 @@ def tile_list_potline_pair_watch_kernel(
 
         def first_products(h):
             e_ps, f_ps = [], []
-            e_all = psum_a.tile([P, PACK, HALF], F32, name="e1", offset=0) if h else None
             for t in range(PACK):
-                acc = e_all[:, t, :] if h else psum_a.tile([P, HALF], F32, name=f"e0{t}", offset=BANK * t)[:]
+                acc = psum_a.tile([P, HALF], F32, name="acc_a")[:]
                 for a in range(2):
                     nc.tensor.matmul_mx(
                         out=acc,
@@ -199,21 +195,25 @@ def tile_list_potline_pair_watch_kernel(
 
         h_bf = [kept(f"h_bf{h}", [P, HALF * PACK], BF16) for h in range(2)]
 
-        def features(h):
+        def features(h, engine_copy, tag):
             e_ps, f_ps = first_products(h)
-            diff = kept(f"diff{h}", [P, PACK, HALF], F32, tag="diff")
+            h_rows = kept(f"h_rows{h}", [P, PACK, HALF], BF16)
+            e_gain = kept(f"e_gain{h}", [P, PACK, HALF], F32, tag=tag)
+            for t in range(PACK):
+                nc.scalar.activation(
+                    out=e_gain[:, t, :], in_=e_ps[t], func=ACT.Copy, scale=gain_t[:, t : t + 1]
+                )
             for t in range(PACK):
                 act = work.tile([P, HALF], F32, name="act")
                 nc.scalar.activation(out=act[:], in_=f_ps[t][:], func=ACT.Silu)
-                nc.vector.tensor_tensor(out=diff[:, t, :], in0=act[:], in1=e_ps[t], op=ALU.subtract)
-            nc.vector.tensor_tensor(
-                out=walk(h_bf[h][:], "p (c i t)"),
-                in0=walk(diff[:], "p t (c i)"),
-                in1=gain_t[:].unsqueeze(1).unsqueeze(3).to_broadcast([P, HALF // 4, PACK, 4]),
-                op=ALU.mult,
-            )
+                nc.vector.scalar_tensor_tensor(
+                    out=h_rows[:, t, :], in0=act[:], scalar=gain_t[:, t : t + 1], in1=e_gain[:, t, :],
+                    op0=ALU.mult, op1=ALU.subtract,
+                )
+            engine_copy(out=walk(h_bf[h][:], "p (c i t)"), in_=walk(h_rows[:], "p t (c i)"))
 
-        features(0)
+        features(0, nc.vector.tensor_copy, "w1_raw0")
+        load_base("w1_raw0")
         w3_raw.append(load_weight("w3_raw1", w3[:, PASS : 2 * PASS], "v_w00"))
         w3_bf = [kept(f"w3_bf{g}", [P, PACK * PASS], BF16) for g in range(2)]
         round_weight(nc.scalar.copy, w3_bf[0], w3_raw[0], 0, P // 2)
@@ -221,34 +221,14 @@ def tile_list_potline_pair_watch_kernel(
         load_base(0)
         h_q = [quantize("hq0", h_bf[0])]
         w3_q = [quantize("w3q0", w3_bf[0])]
-        w4_w, w4_s = deal_fp4("w4", w4_w_raw, w4_s_raw, "v_w10")
+        w4_w, w4_s = deal_fp4("w4", w4_w_raw, w2_s_raw, "v_w10")
 
         g2 = [kept(f"g2_{i}", [P, S], F32) for i in range(8)]
 
-        def offset_left(i, halves):
+        def second_products(i, h):
             g, t = divmod(i, PACK)
-            cols = slice(HALF * halves[0], HALF * (halves[-1] + 1))
-            left_sb = work.tile([P, S], F32, name="left_sb")
-            for h in halves:
-                left = psum_b.tile([P, HALF], F32, name="acc_b")
-                nc.tensor.matmul_mx(
-                    out=left[:],
-                    lhsT=w3_q[g][0][:, P * t : P * (t + 1)].bitcast(FP8X4),
-                    lhsT_scale=w3_q[g][1][:, P * t : P * (t + 1)],
-                    rhs=h_q[h][0][:].bitcast(FP8X4), rhs_scale=h_q[h][1][:],
-                    start=True, stop=True,
-                )
-                nc.scalar.copy(out=left_sb[:, HALF * h : HALF * (h + 1)], in_=left[:])
-            nc.gpsimd.tensor_tensor(
-                out=g2[i][:, cols], in0=left_sb[:, cols], in1=base_t[i][:, cols], op=ALU.add
-            )
-
-        rights = []
-
-        def offset_left_on_vector(i, h):
-            g, t = divmod(i, PACK)
-            cols = slice(HALF * h, HALF * (h + 1))
             left = psum_b.tile([P, HALF], F32, name="acc_b")
+            right = psum_a.tile([P, HALF], F32, name="acc_a")
             nc.tensor.matmul_mx(
                 out=left[:],
                 lhsT=w3_q[g][0][:, P * t : P * (t + 1)].bitcast(FP8X4),
@@ -256,22 +236,28 @@ def tile_list_potline_pair_watch_kernel(
                 rhs=h_q[h][0][:].bitcast(FP8X4), rhs_scale=h_q[h][1][:],
                 start=True, stop=True,
             )
-            nc.vector.tensor_tensor(out=g2[i][:, cols], in0=left[:], in1=base_t[i][:, cols], op=ALU.add)
+            nc.tensor.matmul_mx(
+                out=right[:],
+                lhsT=w4_w[:, g, 2 * P * t : 2 * P * (t + 1)].bitcast(FP4X4),
+                lhsT_scale=w4_s[:, g, P * t : P * (t + 1)],
+                rhs=h_q[h][0][:].bitcast(FP8X4), rhs_scale=h_q[h][1][:],
+                start=True, stop=True,
+            )
+            return left, right
 
-        def times_right(i, halves):
-            g, t = divmod(i, PACK)
-            for h in halves:
-                right = psum_a.tile([P, HALF], F32, name=f"right{i}{h}", offset=BANK * (len(rights) % PACK))
-                rights.append(right)
-                nc.tensor.matmul_mx(
-                    out=right[:],
-                    lhsT=w4_w[:, g, 2 * P * t : 2 * P * (t + 1)].bitcast(FP4X4),
-                    lhsT_scale=w4_s[:, g, P * t : P * (t + 1)],
-                    rhs=h_q[h][0][:].bitcast(FP8X4), rhs_scale=h_q[h][1][:],
-                    start=True, stop=True,
+        def combine(units):
+            banks = [second_products(i, h) for i, h in units]
+            sums = []
+            for (i, h), (left, right) in zip(units, banks):
+                total = work.tile([P, HALF], F32, name="total")
+                nc.vector.tensor_tensor(
+                    out=total[:], in0=left[:], in1=base_t[i][:, HALF * h : HALF * (h + 1)], op=ALU.add
                 )
-                part = g2[i][:, HALF * h : HALF * (h + 1)]
-                nc.vector.tensor_tensor(out=part, in0=right[:], in1=part, op=ALU.mult)
+                sums.append(total)
+            for (i, h), (left, right), total in zip(units, banks, sums):
+                nc.vector.tensor_tensor(
+                    out=g2[i][:, HALF * h : HALF * (h + 1)], in0=right[:], in1=total[:], op=ALU.mult
+                )
 
         y = [kept(f"y{g}", [P, PACK, PAIRS], F32) for g in range(2)]
         y_bf = [kept(f"y_bf{g}", [P, PAIRS * PACK], BF16) for g in range(2)]
@@ -331,32 +317,27 @@ def tile_list_potline_pair_watch_kernel(
                 )
 
         mid = PAIRS // 2
-        for i in range(PACK):
-            offset_left(i, [0])
-        features(1)
+        features(1, nc.scalar.copy, None)
         load_base("tab_s")
         h_q.append(quantize("hq1", h_bf[1]))
-        offset_left_on_vector(0, 1)
-        for i in range(PACK):
-            times_right(i, [0])
-        offset_left(1, [1])
+        combine([(0, 0), (1, 0)])
         round_weight(nc.scalar.copy, w3_bf[1], w3_raw[1], 0, P // 2)
         round_weight(nc.scalar.copy, w3_bf[1], w3_raw[1], P // 2, P)
-        w3_q.append(quantize("w3q1", w3_bf[1]))
-        for i in range(8):
-            if i + 2 < 8:
-                offset_left(i + 2, [1] if i + 2 < PACK else [0, 1])
-            times_right(i, [1] if i < PACK else [0, 1])
-            if i < 7:
-                pick_both(i)
-            if i == 4:
-                round_y(0, nc.scalar.copy, 0, mid)
-            if i == 5:
-                round_y(0, nc.scalar.copy, mid, PAIRS)
+        combine([(0, 1), (1, 1)])
+        for i in range(2, 2 * PACK):
+            pick_both(i - 2)
+            if i == 3:
+                w3_q.append(quantize("w3q1", w3_bf[1]))
             if i == 6:
-                quantize_y(0, 0, PAIRS)
-                store_scales(0)
+                round_y(0, nc.scalar.copy, 0, mid)
+            if i == 7:
+                round_y(0, nc.scalar.copy, mid, PAIRS)
+            combine([(i, 0), (i, 1)])
+        pick_paired(6)
+        quantize_y(0, 0, PAIRS)
+        store_scales(0)
         pick_paired(7, 0, mid)
+        pick_first(6)
         pick_paired(7, mid, PAIRS)
         pick_first(7, 0, mid)
         round_y(1, nc.scalar.copy, 0, mid)

@@ -34,7 +34,7 @@ def tile_list_potline_pair_watch_kernel(
         staged = ctx.enter_context(tc.tile_pool(name="staged", bufs=1))
         work = ctx.enter_context(tc.tile_pool(name="work", bufs=4))
         psum_a = ctx.enter_context(tc.psum_pool(name="psum_a", bufs=4))
-        psum_b = ctx.enter_context(tc.psum_pool(name="psum_b", bufs=4))
+        psum_b = ctx.enter_context(tc.psum_pool(name="psum_b", bufs=2))
 
         def kept(name, shape, dtype, tag=None):
             if isinstance(tag, int):
@@ -61,7 +61,7 @@ def tile_list_potline_pair_watch_kernel(
                 in_=tab_scales[:, 4 * q : 4 * q + 4, :].bitcast(I32),
             )
         nc.scalar.activation(out=warm_out[:], in_=warm_in[:], func=ACT.Silu)
-        tab_w = [kept("tab_w0", [P, T], U32, tag=1024), kept("tab_w1", [P, T], U32)]
+        tab_w = [kept("tab_w0", [P, T], U32, tag=7680), kept("tab_w1", [P, T], U32)]
         for a in range(2):
             nc.sync.dma_start(
                 out=tab_w[a][:].bitcast(I32),
@@ -95,12 +95,6 @@ def tile_list_potline_pair_watch_kernel(
                 nc.sync.dma_start(out=both[:, u, :], in_=rows[:, t + u, :])
                 base_t.append(both[:, u, :])
 
-        v_s0 = kept("v_s0", [P, S], U8)
-        v_s1 = kept("v_s1", [P, S], U8)
-        nc.vector.tensor_copy(out=v_s0[:], in_=tab_s[:].indirect(offs_t[:]))
-        nc.sync.dma_start(out=v_s1[0:100, :].bitcast(I32), in_=v_s0[4:104, :].bitcast(I32))
-        v_s_fp4 = [v_s0[:], v_s1[:]]
-        v_s_fp8 = [v_s0[:], v_s0[4:128]]
         w1_raw = [load_weight("w1_raw0", w1[0:PASS, :], "w1_raw0")]
         v_w = {}
 
@@ -124,8 +118,8 @@ def tile_list_potline_pair_watch_kernel(
 
         def round_weight(engine_copy, grouped, raw, m0, m1):
             engine_copy(
-                out=grouped[:].rearrange("p (t m j) -> p m j t", t=PACK, j=PACK)[:, m0:m1],
-                in_=raw[:].rearrange("p j (m t) -> p m j t", t=PACK)[:, m0:m1],
+                out=grouped[:].rearrange("p (t m j) -> p m t j", t=PACK, j=PACK)[:, m0:m1],
+                in_=raw[:].rearrange("p j (m t) -> p m t j", t=PACK)[:, m0:m1],
             )
 
         def quantize(name, grouped):
@@ -134,12 +128,18 @@ def tile_list_potline_pair_watch_kernel(
             nc.vector.quantize_mx(out=words[:].bitcast(FP8X4), scales=scales[:], in_=grouped[:])
             return words, scales
 
-        w1_raw.append(load_weight("w1_raw1", w1[PASS : 2 * PASS, :], "tab_s"))
         gather_words(0, 0)
         gather_words(0, 1)
-        w3_raw = [load_weight("w3_raw0", w3[:, 0:PASS], 0)]
+        w1_raw.append(load_weight("w1_raw1", w1[PASS : 2 * PASS, :], 0))
+        v_s0 = kept("v_s0", [P, S], U8, tag=10240)
+        v_s1 = kept("v_s1", [P, S], U8)
+        nc.vector.tensor_copy(out=v_s0[:], in_=tab_s[:].indirect(offs_t[:]))
+        nc.sync.dma_start(out=v_s1[0:100, :].bitcast(I32), in_=v_s0[4:104, :].bitcast(I32))
+        v_s_fp4 = [v_s0[:], v_s1[:]]
+        v_s_fp8 = [v_s0[:], v_s0[4:128]]
+        w3_raw = [load_weight("w3_raw0", w3[:, 0:PASS], "tab_s")]
+        w2_w, w2_s = deal_fp4("w2", w2_w_raw, w2_s_raw, 9216)
         gather_words(1, 0)
-        w2_w, w2_s = deal_fp4("w2", w2_w_raw, w2_s_raw, 8192)
         w4_w_raw = kept("w4_w_raw", [P, 2, 2 * PASS], U8, tag="w2_w_raw")
         nc.sync.dma_start(
             out=w4_w_raw[:].rearrange("p g c -> p (g c)").bitcast(I32), in_=w4_words[0].bitcast(I32)
@@ -156,36 +156,34 @@ def tile_list_potline_pair_watch_kernel(
         round_weight(nc.vector.tensor_copy, w1_bf[1], w1_raw[1], 0, VECTOR_M)
         round_weight(nc.scalar.copy, w1_bf[1], w1_raw[1], VECTOR_M, P)
         w1_q.append(quantize("w1q1", w1_bf[1]))
-        gather_words(1, 1, tag="tab_s")
+        gather_words(1, 1, tag=0)
         share_t = kept("share_t", [P, 2, PACK], F32, tag="w1_bf1")
         nc.sync.dma_start(out=share_t[:], in_=share.rearrange("(g p t) -> p g t", g=2, t=PACK))
         load_base("tab_w1")
 
         def first_products(h):
-            e_ps, f_ps = [], []
-            for t in range(PACK):
-                acc = psum_a.tile([P, HALF], F32, name="acc_a")[:]
-                for a in range(2):
+            cols = slice(HALF * h, HALF * (h + 1))
+            e_ps = [psum_a.tile([P, HALF], F32, name="acc_a") for t in range(PACK)]
+            for a in range(2):
+                for t in range(PACK):
                     nc.tensor.matmul_mx(
-                        out=acc,
+                        out=e_ps[t][:],
                         lhsT=w2_w[:, a, 2 * P * t : 2 * P * (t + 1)].bitcast(FP4X4),
                         lhsT_scale=w2_s[:, a, P * t : P * (t + 1)],
                         rhs=v_w[a, h][:].bitcast(FP8X4),
-                        rhs_scale=v_s_fp4[a][:, HALF * h : HALF * (h + 1)],
+                        rhs_scale=v_s_fp4[a][:, cols],
                         start=(a == 0), stop=(a == 1),
                     )
-                e_ps.append(acc)
-            steps = [(a, t) for t in range(PACK) for a in range(2)]
-            for a, t in sorted(steps) if h == 0 else steps:
-                if a == 0:
-                    f_ps.append(psum_b.tile([P, HALF], F32, name="acc_b"))
-                if True:
+            f_ps = []
+            for t in range(PACK):
+                f_ps.append(psum_b.tile([P, HALF], F32, name="acc_c" if h == 0 and t >= 2 else "acc_b"))
+                for a in range(2):
                     nc.tensor.matmul_mx(
                         out=f_ps[t][:],
                         lhsT=w1_q[a][0][:, P * t : P * (t + 1)].bitcast(FP8X4),
                         lhsT_scale=w1_q[a][1][:, P * t : P * (t + 1)],
                         rhs=v_w[a, h][:].bitcast(FP8X4),
-                        rhs_scale=v_s_fp8[a][:, HALF * h : HALF * (h + 1)],
+                        rhs_scale=v_s_fp8[a][:, cols],
                         start=(a == 0), stop=(a == 1),
                     )
             return e_ps, f_ps
@@ -201,7 +199,7 @@ def tile_list_potline_pair_watch_kernel(
             e_gain = kept(f"e_gain{h}", [P, PACK, HALF], F32, tag=tag)
             for t in range(PACK):
                 nc.scalar.activation(
-                    out=e_gain[:, t, :], in_=e_ps[t], func=ACT.Copy, scale=gain_t[:, t : t + 1]
+                    out=e_gain[:, t, :], in_=e_ps[t][:], func=ACT.Copy, scale=gain_t[:, t : t + 1]
                 )
             for t in range(PACK):
                 act = work.tile([P, HALF], F32, name="act")
@@ -218,17 +216,16 @@ def tile_list_potline_pair_watch_kernel(
         w3_bf = [kept(f"w3_bf{g}", [P, PACK * PASS], BF16) for g in range(2)]
         round_weight(nc.scalar.copy, w3_bf[0], w3_raw[0], 0, P // 2)
         round_weight(nc.scalar.copy, w3_bf[0], w3_raw[0], P // 2, P)
-        load_base(0)
+        load_base("tab_s")
         h_q = [quantize("hq0", h_bf[0])]
         w3_q = [quantize("w3q0", w3_bf[0])]
         w4_w, w4_s = deal_fp4("w4", w4_w_raw, w2_s_raw, "v_w10")
 
         g2 = [kept(f"g2_{i}", [P, S], F32) for i in range(8)]
 
-        def second_products(i, h):
+        def left_product(i, h):
             g, t = divmod(i, PACK)
-            left = psum_b.tile([P, HALF], F32, name="acc_b")
-            right = psum_a.tile([P, HALF], F32, name="acc_a")
+            left = psum_b.tile([P, HALF], F32, name="acc_b" if h else "acc_c")
             nc.tensor.matmul_mx(
                 out=left[:],
                 lhsT=w3_q[g][0][:, P * t : P * (t + 1)].bitcast(FP8X4),
@@ -236,6 +233,23 @@ def tile_list_potline_pair_watch_kernel(
                 rhs=h_q[h][0][:].bitcast(FP8X4), rhs_scale=h_q[h][1][:],
                 start=True, stop=True,
             )
+            return left
+
+        def add_base(i, h):
+            cols = slice(HALF * h, HALF * (h + 1))
+            left = left_product(i, h)
+            nc.vector.tensor_tensor(out=g2[i][:, cols], in0=left[:], in1=base_t[i][:, cols], op=ALU.add)
+
+        def add_base_aside(i, h):
+            cols = slice(HALF * h, HALF * (h + 1))
+            left = left_product(i, h)
+            left_sb = work.tile([P, HALF], F32, name="left_sb")
+            nc.scalar.copy(out=left_sb[:], in_=left[:])
+            nc.gpsimd.tensor_tensor(out=g2[i][:, cols], in0=left_sb[:], in1=base_t[i][:, cols], op=ALU.add)
+
+        def times_right(i, h):
+            g, t = divmod(i, PACK)
+            right = psum_a.tile([P, HALF], F32, name="acc_a")
             nc.tensor.matmul_mx(
                 out=right[:],
                 lhsT=w4_w[:, g, 2 * P * t : 2 * P * (t + 1)].bitcast(FP4X4),
@@ -243,21 +257,8 @@ def tile_list_potline_pair_watch_kernel(
                 rhs=h_q[h][0][:].bitcast(FP8X4), rhs_scale=h_q[h][1][:],
                 start=True, stop=True,
             )
-            return left, right
-
-        def combine(units):
-            banks = [second_products(i, h) for i, h in units]
-            sums = []
-            for (i, h), (left, right) in zip(units, banks):
-                total = work.tile([P, HALF], F32, name="total")
-                nc.vector.tensor_tensor(
-                    out=total[:], in0=left[:], in1=base_t[i][:, HALF * h : HALF * (h + 1)], op=ALU.add
-                )
-                sums.append(total)
-            for (i, h), (left, right), total in zip(units, banks, sums):
-                nc.vector.tensor_tensor(
-                    out=g2[i][:, HALF * h : HALF * (h + 1)], in0=right[:], in1=total[:], op=ALU.mult
-                )
+            part = g2[i][:, HALF * h : HALF * (h + 1)]
+            nc.vector.tensor_tensor(out=part, in0=right[:], in1=part, op=ALU.mult)
 
         y = [kept(f"y{g}", [P, PACK, PAIRS], F32) for g in range(2)]
         y_bf = [kept(f"y_bf{g}", [P, PAIRS * PACK], BF16) for g in range(2)]
@@ -318,21 +319,36 @@ def tile_list_potline_pair_watch_kernel(
 
         mid = PAIRS // 2
         features(1, nc.scalar.copy, None)
-        load_base("tab_s")
+        load_base(0)
         h_q.append(quantize("hq1", h_bf[1]))
-        combine([(0, 0), (1, 0)])
+        for pair in ((0, 1), (2, 3)):
+            for i in pair:
+                add_base(i, 0)
+            for i in pair:
+                times_right(i, 0)
+        add_base(0, 1)
+        add_base_aside(1, 1)
+        add_base_aside(2, 1)
+        times_right(0, 1)
         round_weight(nc.scalar.copy, w3_bf[1], w3_raw[1], 0, P // 2)
         round_weight(nc.scalar.copy, w3_bf[1], w3_raw[1], P // 2, P)
-        combine([(0, 1), (1, 1)])
+        pick_both(0)
+        times_right(1, 1)
+        w3_q.append(quantize("w3q1", w3_bf[1]))
         for i in range(2, 2 * PACK):
-            pick_both(i - 2)
-            if i == 3:
-                w3_q.append(quantize("w3q1", w3_bf[1]))
-            if i == 6:
+            if i + 1 < 2 * PACK:
+                add_base_aside(i + 1, 1)
+            if i >= PACK:
+                add_base(i, 0)
+            times_right(i, 1)
+            if i >= PACK:
+                times_right(i, 0)
+            if i < 2 * PACK - 1:
+                pick_both(i - 1)
+            if i == 5:
                 round_y(0, nc.scalar.copy, 0, mid)
-            if i == 7:
+            if i == 6:
                 round_y(0, nc.scalar.copy, mid, PAIRS)
-            combine([(i, 0), (i, 1)])
         pick_paired(6)
         quantize_y(0, 0, PAIRS)
         store_scales(0)

from contextlib import ExitStack

import concourse.mybir as mybir

K, T, S, H, N, PAIRS = 1024, 2048, 1024, 512, 1024, 512
FLOPS = 2 * (2 * K * H * S + 2 * H * N * S)

F32 = mybir.dt.float32
BF16 = mybir.dt.bfloat16
I32 = mybir.dt.int32
U32 = mybir.dt.uint32
U16 = mybir.dt.uint16
U8 = mybir.dt.uint8
FP8X4 = mybir.dt.float8_e4m3fn_x4
FP4X4 = mybir.dt.float4_e2m1fn_x4
ACT = mybir.ActivationFunctionType
ALU = mybir.AluOpType

P = 128
PACK = 4
PASS = P * PACK
HALF = 512
BANK = 2048
VECTOR_M = 96


def tile_list_potline_pair_watch_kernel(
    tc, tab_words, tab_scales, offs, w1, w2_words, w2_scales, gain, w3, base,
    w4_words, w4_scales, pos1, pos2, share, out_0, out_1, out_2,
):
    nc = tc.nc
    with ExitStack() as ctx:
        keep = ctx.enter_context(tc.tile_pool(name="keep", bufs=1))
        staged = ctx.enter_context(tc.tile_pool(name="staged", bufs=1))
        work = ctx.enter_context(tc.tile_pool(name="work", bufs=4))
        psum_a = ctx.enter_context(tc.psum_pool(name="psum_a", bufs=4))
        psum_b = ctx.enter_context(tc.psum_pool(name="psum_b", bufs=2))

        def kept(name, shape, dtype, tag=None):
            if isinstance(tag, int):
                return staged.tile(shape, dtype, name=name, align_bytes=64, offset=tag)
            return keep.tile(shape, dtype, name=name, tag=tag or name, align_bytes=64)

        offs_t = keep.tile([P, S // 16], U16, name="offs_t")
        pos1_t = keep.tile([P, PAIRS // 16], U16, name="pos1_t")
        pos2_t = keep.tile([P, PAIRS // 16], U16, name="pos2_t")
        tab_s = kept("tab_s", [P, T], U8)
        w2_s_raw = kept("w2_s_raw", [P, 2, PASS], U8)
        warm_in = kept("warm_in", [P, 1], F32)
        warm_out = kept("warm_out", [P, 1], F32)
        nc.vector.memset(tab_s[:].bitcast(I32), 0)
        nc.gpsimd.memset(w2_s_raw[:].bitcast(I32), 0)
        nc.vector.memset(warm_in[:], 0.0)

        nc.sync.dma_start(offs_t[:], offs)
        nc.sync.dma_start(pos1_t[:], pos1)
        nc.sync.dma_start(pos2_t[:], pos2)
        for q in range(4):
            nc.scalar.dma_start(
                out=tab_s[32 * q : 32 * q + 8, :].bitcast(I32),
                in_=tab_scales[:, 4 * q : 4 * q + 4, :].bitcast(I32),
            )
        nc.scalar.activation(out=warm_out[:], in_=warm_in[:], func=ACT.Silu)
        tab_w = [kept("tab_w0", [P, T], U32, tag=7680), kept("tab_w1", [P, T], U32)]
        for a in range(2):
            nc.sync.dma_start(
                out=tab_w[a][:].bitcast(I32),
                in_=tab_words[a].rearrange("p t i -> p (t i)").bitcast(I32),
            )
        w2_w_raw = kept("w2_w_raw", [P, 2, 2 * PASS], U8)
        nc.sync.dma_start(
            out=w2_w_raw[:].bitcast(I32), in_=w2_words.rearrange("a p c -> p a c").bitcast(I32)
        )
        for q in range(4):
            nc.gpsimd.dma_start(
                out=w2_s_raw[32 * q : 32 * q + 4].bitcast(I32),
                in_=w2_scales[:, 4 * q : 4 * q + 4, :].rearrange("a r c -> r a c").bitcast(I32),
            )
        gain_t = kept("gain_t", [P, PACK], F32, tag="warm_in")
        nc.sync.dma_start(out=gain_t[:], in_=gain.rearrange("(p t) -> p t", t=PACK))

        def load_weight(name, rows, tag):
            raw = kept(name, [P, PACK, PASS], F32, tag=tag)
            nc.sync.dma_start(out=raw[:], in_=rows.rearrange("(p j) c -> p j c", j=PACK))
            return raw

        base_t = []

        def load_base(tag):
            pair = len(base_t) // 2
            g, t = divmod(2 * pair, PACK)
            rows = base[PASS * g : PASS * (g + 1), :].rearrange("(p t) j -> p t j", t=PACK)
            both = kept(f"base{pair}", [P, 2, S], F32, tag=tag)
            for u in range(2):
                nc.sync.dma_start(out=both[:, u, :], in_=rows[:, t + u, :])
                base_t.append(both[:, u, :])

        w1_raw = [load_weight("w1_raw0", w1[0:PASS, :], "w1_raw0")]
        v_w = {}

        def gather_words(a, h, tag=None):
            v_w[a, h] = kept(f"v_w{a}{h}", [P, HALF], U32, tag=tag)
            cols = offs_t[:, 32 * h : 32 * (h + 1)]
            nc.vector.tensor_copy(out=v_w[a, h][:], in_=tab_w[a][:].indirect(cols))

        def deal_fp4(name, words_raw, scales_raw, tag):
            words = kept(name + "_w", [P, 2, 2 * PASS], U8)
            scales = kept(name + "_s", [P, 2, PASS], U8, tag=tag)
            nc.vector.tensor_copy(
                out=words[:].bitcast(U16).rearrange("p a (t m) -> p a t m", t=PACK),
                in_=words_raw[:].bitcast(U16).rearrange("p a (m t) -> p a t m", t=PACK),
            )
            nc.vector.tensor_copy(
                out=scales[:].rearrange("p a (t m) -> p a t m", t=PACK),
                in_=scales_raw[:].rearrange("p a (m t) -> p a t m", t=PACK),
            )
            return words, scales

        def round_weight(engine_copy, grouped, raw, m0, m1):
            engine_copy(
                out=grouped[:].rearrange("p (t m j) -> p m t j", t=PACK, j=PACK)[:, m0:m1],
                in_=raw[:].rearrange("p j (m t) -> p m t j", t=PACK)[:, m0:m1],
            )

        def quantize(name, grouped):
            words = kept(name + "_w", [P, PASS], U32)
            scales = kept(name + "_s", [P, PASS], U8)
            nc.vector.quantize_mx(out=words[:].bitcast(FP8X4), scales=scales[:], in_=grouped[:])
            return words, scales

        gather_words(0, 0)
        gather_words(0, 1)
        w1_raw.append(load_weight("w1_raw1", w1[PASS : 2 * PASS, :], 0))
        v_s0 = kept("v_s0", [P, S], U8, tag=10240)
        v_s1 = kept("v_s1", [P, S], U8)
        nc.vector.tensor_copy(out=v_s0[:], in_=tab_s[:].indirect(offs_t[:]))
        nc.sync.dma_start(out=v_s1[0:100, :].bitcast(I32), in_=v_s0[4:104, :].bitcast(I32))
        v_s_fp4 = [v_s0[:], v_s1[:]]
        v_s_fp8 = [v_s0[:], v_s0[4:128]]
        w3_raw = [load_weight("w3_raw0", w3[:, 0:PASS], "tab_s")]
        w2_w, w2_s = deal_fp4("w2", w2_w_raw, w2_s_raw, 9216)
        gather_words(1, 0)
        w4_w_raw = kept("w4_w_raw", [P, 2, 2 * PASS], U8, tag="w2_w_raw")
        nc.sync.dma_start(
            out=w4_w_raw[:].rearrange("p g c -> p (g c)").bitcast(I32), in_=w4_words[0].bitcast(I32)
        )
        for q in range(4):
            nc.sync.dma_start(
                out=w2_s_raw[32 * q : 32 * q + 4].rearrange("r g c -> r (g c)").bitcast(I32),
                in_=w4_scales[0, 4 * q : 4 * q + 4, :].bitcast(I32),
            )

        w1_bf = [kept(f"w1_bf{a}", [P, PACK * H], BF16) for a in range(2)]
        round_weight(nc.scalar.copy, w1_bf[0], w1_raw[0], 0, P)
        w1_q = [quantize("w1q0", w1_bf[0])]
        round_weight(nc.vector.tensor_copy, w1_bf[1], w1_raw[1], 0, VECTOR_M)
        round_weight(nc.scalar.copy, w1_bf[1], w1_raw[1], VECTOR_M, P)
        w1_q.append(quantize("w1q1", w1_bf[1]))
        gather_words(1, 1, tag=0)
        share_t = kept("share_t", [P, 2, PACK], F32, tag="w1_bf1")
        nc.sync.dma_start(out=share_t[:], in_=share.rearrange("(g p t) -> p g t", g=2, t=PACK))
        load_base("tab_w1")

        def first_products(h):
            cols = slice(HALF * h, HALF * (h + 1))
            e_ps = [psum_a.tile([P, HALF], F32, name="acc_a") for t in range(PACK)]
            for a in range(2):
                for t in range(PACK):
                    nc.tensor.matmul_mx(
                        out=e_ps[t][:],
                        lhsT=w2_w[:, a, 2 * P * t : 2 * P * (t + 1)].bitcast(FP4X4),
                        lhsT_scale=w2_s[:, a, P * t : P * (t + 1)],
                        rhs=v_w[a, h][:].bitcast(FP8X4),
                        rhs_scale=v_s_fp4[a][:, cols],
                        start=(a == 0), stop=(a == 1),
                    )
            f_ps = []
            for t in range(PACK):
                f_ps.append(psum_b.tile([P, HALF], F32, name="acc_c" if h == 0 and t >= 2 else "acc_b"))
                for a in range(2):
                    nc.tensor.matmul_mx(
                        out=f_ps[t][:],
                        lhsT=w1_q[a][0][:, P * t : P * (t + 1)].bitcast(FP8X4),
                        lhsT_scale=w1_q[a][1][:, P * t : P * (t + 1)],
                        rhs=v_w[a, h][:].bitcast(FP8X4),
                        rhs_scale=v_s_fp8[a][:, cols],
                        start=(a == 0), stop=(a == 1),
                    )
            return e_ps, f_ps

        def walk(ap, pattern):
            return ap.rearrange(pattern + " -> p c t i", t=PACK, i=4)

        h_bf = [kept(f"h_bf{h}", [P, HALF * PACK], BF16) for h in range(2)]

        def features(h, engine_copy, tag):
            e_ps, f_ps = first_products(h)
            h_rows = kept(f"h_rows{h}", [P, PACK, HALF], BF16)
            e_gain = kept(f"e_gain{h}", [P, PACK, HALF], F32, tag=tag)
            for t in range(PACK):
                nc.scalar.activation(
                    out=e_gain[:, t, :], in_=e_ps[t][:], func=ACT.Copy, scale=gain_t[:, t : t + 1]
                )
            for t in range(PACK):
                act = work.tile([P, HALF], F32, name="act")
                nc.scalar.activation(out=act[:], in_=f_ps[t][:], func=ACT.Silu)
                nc.vector.scalar_tensor_tensor(
                    out=h_rows[:, t, :], in0=act[:], scalar=gain_t[:, t : t + 1], in1=e_gain[:, t, :],
                    op0=ALU.mult, op1=ALU.subtract,
                )
            engine_copy(out=walk(h_bf[h][:], "p (c i t)"), in_=walk(h_rows[:], "p t (c i)"))

        features(0, nc.vector.tensor_copy, "w1_raw0")
        load_base("w1_raw0")
        w3_raw.append(load_weight("w3_raw1", w3[:, PASS : 2 * PASS], "v_w00"))
        w3_bf = [kept(f"w3_bf{g}", [P, PACK * PASS], BF16) for g in range(2)]
        round_weight(nc.scalar.copy, w3_bf[0], w3_raw[0], 0, P // 2)
        round_weight(nc.scalar.copy, w3_bf[0], w3_raw[0], P // 2, P)
        load_base("tab_s")
        h_q = [quantize("hq0", h_bf[0])]
        w3_q = [quantize("w3q0", w3_bf[0])]
        w4_w, w4_s = deal_fp4("w4", w4_w_raw, w2_s_raw, "v_w10")

        g2 = [kept(f"g2_{i}", [P, S], F32) for i in range(8)]

        def left_product(i, h):
            g, t = divmod(i, PACK)
            left = psum_b.tile([P, HALF], F32, name="acc_b" if h else "acc_c")
            nc.tensor.matmul_mx(
                out=left[:],
                lhsT=w3_q[g][0][:, P * t : P * (t + 1)].bitcast(FP8X4),
                lhsT_scale=w3_q[g][1][:, P * t : P * (t + 1)],
                rhs=h_q[h][0][:].bitcast(FP8X4), rhs_scale=h_q[h][1][:],
                start=True, stop=True,
            )
            return left

        def add_base(i, h):
            cols = slice(HALF * h, HALF * (h + 1))
            left = left_product(i, h)
            nc.vector.tensor_tensor(out=g2[i][:, cols], in0=left[:], in1=base_t[i][:, cols], op=ALU.add)

        def add_base_aside(i, h):
            cols = slice(HALF * h, HALF * (h + 1))
            left = left_product(i, h)
            left_sb = work.tile([P, HALF], F32, name="left_sb")
            nc.scalar.copy(out=left_sb[:], in_=left[:])
            nc.gpsimd.tensor_tensor(out=g2[i][:, cols], in0=left_sb[:], in1=base_t[i][:, cols], op=ALU.add)

        def times_right(i, h):
            g, t = divmod(i, PACK)
            right = psum_a.tile([P, HALF], F32, name="acc_a")
            nc.tensor.matmul_mx(
                out=right[:],
                lhsT=w4_w[:, g, 2 * P * t : 2 * P * (t + 1)].bitcast(FP4X4),
                lhsT_scale=w4_s[:, g, P * t : P * (t + 1)],
                rhs=h_q[h][0][:].bitcast(FP8X4), rhs_scale=h_q[h][1][:],
                start=True, stop=True,
            )
            part = g2[i][:, HALF * h : HALF * (h + 1)]
            nc.vector.tensor_tensor(out=part, in0=right[:], in1=part, op=ALU.mult)

        y = [kept(f"y{g}", [P, PACK, PAIRS], F32) for g in range(2)]
        y_bf = [kept(f"y_bf{g}", [P, PAIRS * PACK], BF16) for g in range(2)]
        y_w = [kept(f"y_w{g}", [P, PAIRS], U32) for g in range(2)]
        y_s = [kept(f"y_s{g}", [P, PAIRS], U8) for g in range(2)]
        scaled = {}

        def pick_paired(i, m0=0, m1=PAIRS):
            g, t = divmod(i, PACK)
            paired = work.tile([P, m1 - m0], F32, name="paired", bufs=3)
            nc.vector.tensor_copy(out=paired[:], in_=g2[i][:].indirect(pos2_t[:, m0 // 16 : m1 // 16]))
            scaled[i, m0] = work.tile([P, m1 - m0], F32, name="scaled", bufs=3)
            nc.scalar.activation(
                out=scaled[i, m0][:], in_=paired[:], func=ACT.Copy, scale=share_t[:, g, t : t + 1]
            )

        def pick_first(i, m0=0, m1=PAIRS):
            g, t = divmod(i, PACK)
            nc.vector.tensor_tensor(
                out=y[g][:, t, m0:m1], in0=g2[i][:].indirect(pos1_t[:, m0 // 16 : m1 // 16]),
                in1=scaled[i, m0][:], op=ALU.subtract,
            )
            rows = out_0[PASS * g : PASS * (g + 1), :].rearrange("(p t) m -> p t m", t=PACK)
            nc.sync.dma_start(out=rows[:, t, m0:m1], in_=y[g][:, t, m0:m1])

        def pick_both(i):
            g, t = divmod(i, PACK)
            pick_paired(i)
            first = work.tile([P, PAIRS], F32, name="first", bufs=3)
            nc.vector.tensor_copy(out=first[:], in_=g2[i][:].indirect(pos1_t[:]))
            nc.gpsimd.tensor_tensor(
                out=y[g][:, t, :], in0=first[:], in1=scaled[i, 0][:], op=ALU.subtract
            )
            rows = out_0[PASS * g : PASS * (g + 1), :].rearrange("(p t) m -> p t m", t=PACK)
            nc.sync.dma_start(out=rows[:, t, :], in_=y[g][:, t, :])

        def round_y(g, engine_copy, m0, m1):
            engine_copy(
                out=walk(y_bf[g][:, PACK * m0 : PACK * m1], "p (c i t)"),
                in_=walk(y[g][:, :, m0:m1], "p t (c i)"),
            )

        def quantize_y(g, m0, m1):
            nc.vector.quantize_mx(
                out=y_w[g][:, m0:m1].bitcast(FP8X4), scales=y_s[g][:, m0:m1],
                in_=y_bf[g][:, PACK * m0 : PACK * m1],
            )
            words = out_1[g].rearrange("p m t -> p (m t)").bitcast(I32)
            nc.sync.dma_start(out=words[:, m0:m1], in_=y_w[g][:, m0:m1].bitcast(I32))

        def store_scales(g):
            for q in range(4):
                queue = nc.scalar if q % 2 else nc.sync
                queue.dma_start(
                    out=out_2[g, 4 * q : 4 * q + 4, :].bitcast(I32),
                    in_=y_s[g][32 * q : 32 * q + 4, :].bitcast(I32),
                )

        mid = PAIRS // 2
        features(1, nc.scalar.copy, None)
        load_base(0)
        h_q.append(quantize("hq1", h_bf[1]))
        for pair in ((0, 1), (2, 3)):
            for i in pair:
                add_base(i, 0)
            for i in pair:
                times_right(i, 0)
        add_base(0, 1)
        add_base_aside(1, 1)
        add_base_aside(2, 1)
        times_right(0, 1)
        round_weight(nc.scalar.copy, w3_bf[1], w3_raw[1], 0, P // 2)
        round_weight(nc.scalar.copy, w3_bf[1], w3_raw[1], P // 2, P)
        pick_both(0)
        times_right(1, 1)
        w3_q.append(quantize("w3q1", w3_bf[1]))
        for i in range(2, 2 * PACK):
            if i + 1 < 2 * PACK:
                add_base_aside(i + 1, 1)
            if i >= PACK:
                add_base(i, 0)
            times_right(i, 1)
            if i >= PACK:
                times_right(i, 0)
            if i < 2 * PACK - 1:
                pick_both(i - 1)
            if i == 5:
                round_y(0, nc.scalar.copy, 0, mid)
            if i == 6:
                round_y(0, nc.scalar.copy, mid, PAIRS)
        pick_paired(6)
        quantize_y(0, 0, PAIRS)
        store_scales(0)
        pick_paired(7, 0, mid)
        pick_first(6)
        pick_paired(7, mid, PAIRS)
        pick_first(7, 0, mid)
        round_y(1, nc.scalar.copy, 0, mid)
        pick_first(7, mid, PAIRS)
        round_y(1, nc.vector.tensor_copy, mid, PAIRS)
        quantize_y(1, 0, mid)
        quantize_y(1, mid, PAIRS)
        store_scales(1)
